import numpy as np
import ml_dtypes


def mxq(x, axis, fmt="e4m3"):
    dtype, down = {"e4m3": (ml_dtypes.float8_e4m3fn, 7), "e5m2": (ml_dtypes.float8_e5m2, 14)}[fmt]
    v = np.moveaxis(np.asarray(x, np.float32).astype(ml_dtypes.bfloat16).astype(np.float64), axis, -1)
    blocks = v.reshape(v.shape[:-1] + (-1, 32))
    amax = np.abs(blocks).max(-1, keepdims=True)
    byte = np.maximum(np.where(amax > 0, np.frexp(amax)[1] - 1 + 127, 0) - down, 1)
    scale = np.exp2(byte - 127.0)
    codes = (blocks / scale).astype(np.float32).astype(dtype).astype(np.float64)
    return np.moveaxis((codes * scale).reshape(v.shape), -1, axis)


WIDE = False


def mx_kscale(k):
    if not WIDE:
        return np.ones(k)
    levels = np.array([10, -10, 5, -5, 0])
    if k % 512:
        return np.exp2(np.random.permutation(np.resize(levels, k // 32))).repeat(32)
    a = np.empty((k // 512, 16))
    for p in range(k // 512):
        a[p, :8] = np.random.permutation(np.resize(levels, 8))
        for g in range(8):
            far = levels[np.abs(levels - a[p, g]) >= 10]
            a[p, g + 8] = far[np.random.randint(len(far))]
    return np.exp2(a.ravel()).repeat(32)


def f64(x):
    return np.asarray(x).astype(np.float64)


def striped(idx):
    return np.tile(idx.reshape(-1, 16).T, (8, 1)).astype(np.uint16)


def unstriped(offs):
    return offs[:16].T.reshape(-1).astype(np.int64)


E2M1 = np.array([0.0, 0.5, 1.0, 1.5, 2.0, 3.0, 4.0, 6.0, -0.0, -0.5, -1.0, -1.5, -2.0, -3.0, -4.0, -6.0])


def pack_weight(w, fmt):
    k, n = w.shape
    w = f64(np.asarray(w, np.float32).astype(ml_dtypes.bfloat16)).reshape(k // 32, 32, n)
    amax = np.abs(w).max(1)
    if fmt == "e4m3":
        byte = np.frexp(amax)[1] - 1 + 127 - 7
    else:
        mant, ex = np.frexp(amax / 6.0)
        byte = np.where(mant > 0.5, ex, ex - 1) + 127
    byte = np.clip(np.where(amax > 0, byte, 1), 1, 254)
    scaled = (w * np.exp2(127.0 - byte)[:, None, :]).reshape(k, n).astype(np.float32)
    by_word = np.ascontiguousarray(scaled.reshape(k // 512, 128, 4, n).transpose(0, 1, 3, 2))
    if fmt == "e4m3":
        words = by_word.astype(ml_dtypes.float8_e4m3fn).view(np.uint8)
    else:
        c = by_word.astype(ml_dtypes.float4_e2m1fn).view(np.uint8) & 0xF
        words = (c[..., 0::2] | (c[..., 1::2] << 4)).reshape(k // 512, 128, 2 * n)
    return np.ascontiguousarray(words), np.ascontiguousarray(byte.astype(np.uint8).reshape(k // 512, 16, n))


def unpack_weight(words, scales, fmt):
    g, _, n = scales.shape
    words = np.ascontiguousarray(words).reshape(g, 128, n, -1)
    if fmt == "e4m3":
        vals = words.view(ml_dtypes.float8_e4m3fn).astype(np.float64)
    else:
        nib = np.empty((g, 128, n, 4), np.uint8)
        nib[..., 0::2] = words & 0xF
        nib[..., 1::2] = words >> 4
        vals = E2M1[nib]
    vals = vals * np.repeat(np.exp2(scales.astype(np.float64) - 127.0), 8, axis=1)[..., None]
    return vals.transpose(0, 1, 3, 2).reshape(g * 512, n)


def sigmoid(v):
    return 1.0 / (1.0 + np.exp(-np.maximum(v, -700.0)))


K, T, E, C, H, N = 512, 1280, 4, 256, 1024, 256


def by_expert(wq, xq):
    return np.concatenate([wq[e].T @ xq[:, e * C:(e + 1) * C] for e in range(E)], axis=1)


def setup_inputs():
    n = np.random.standard_normal
    s = mx_kscale(K)[:, None]
    u = mx_kscale(H)
    w1 = [pack_weight(m, "e2m1") for m in n((E, K, H)) / np.sqrt(K) / s[None]]
    w3 = [pack_weight(m, "e2m1") for m in n((E, K, H)) / np.sqrt(K) / s[None] * u[None, None, :]]
    w2 = [pack_weight(m, "e2m1") for m in n((E, H, N)) / np.sqrt(H) / u[None, :, None]]
    return {
        "xT": (n((K, T)) * s).astype(np.float32),
        "xr": n((N, T)).astype(np.float32),
        "w1_words": np.stack([m[0] for m in w1]),
        "w1_scales": np.stack([m[1] for m in w1]),
        "w3_words": np.stack([m[0] for m in w3]),
        "w3_scales": np.stack([m[1] for m in w3]),
        "w2_words": np.stack([m[0] for m in w2]),
        "w2_scales": np.stack([m[1] for m in w2]),
        "gate": np.tile(np.random.uniform(0.2, 1.0, E * C), (N, 1)).astype(np.float32),
        "offs": striped(np.random.permutation(T)[:E * C]),
    }


def reference(xT, xr, w1_words, w1_scales, w3_words, w3_scales, w2_words, w2_scales, gate, offs):
    idx = unstriped(offs)
    w1 = np.stack([unpack_weight(w1_words[e], w1_scales[e], "e2m1") for e in range(E)])
    w3 = np.stack([unpack_weight(w3_words[e], w3_scales[e], "e2m1") for e in range(E)])
    w2 = np.stack([unpack_weight(w2_words[e], w2_scales[e], "e2m1") for e in range(E)])
    xq = mxq(f64(xT)[:, idx], 0, "e4m3")
    h = sigmoid(by_expert(w1, xq))
    h = h * by_expert(w3, xq)
    y = by_expert(w2, mxq(h, 0, "e4m3"))
    out = f64(xr).copy()
    out[:, idx] += f64(gate) * y
    return out

@@ -1,0 +1,218 @@
+from contextlib import ExitStack
+
+import concourse.mybir as mybir
+from concourse.masks import make_identity
+
+K, T, E, C, H, N = 512, 1280, 4, 256, 1024, 256
+FLOPS = 2 * E * C * (2 * K * H + H * N)
+
+F32 = mybir.dt.float32
+BF16 = mybir.dt.bfloat16
+I32 = mybir.dt.int32
+U32 = mybir.dt.uint32
+U16 = mybir.dt.uint16
+U8 = mybir.dt.uint8
+FP8X4 = mybir.dt.float8_e4m3fn_x4
+FP4X4 = mybir.dt.float4_e2m1fn_x4
+SIGMOID = mybir.ActivationFunctionType.Sigmoid
+MULT = mybir.AluOpType.mult
+ADD = mybir.AluOpType.add
+
+P = 128
+PACK = 4
+LOADS = (512, 512, 256)
+CAST = 256
+SCALAR_TOKENS = 96
+HALF = 512
+OUT_PIECE = 640
+
+
+def tile_moe_res_glu_sigmoid_kernel(
+    tc, xT, xr, w1_words, w1_scales, w3_words, w3_scales, w2_words, w2_scales, gate, offs, out
+):
+    nc = tc.nc
+    with ExitStack() as ctx:
+        keep = ctx.enter_context(tc.tile_pool(name="keep", bufs=1))
+        ring = ctx.enter_context(tc.tile_pool(name="ring", bufs=3))
+        psum = ctx.enter_context(tc.psum_pool(name="psum", bufs=2))
+
+        warm = keep.tile([P, 1], F32, name="warm")
+        nc.vector.memset(warm[:], 0.0)
+        warmed = keep.tile([P, 1], F32, name="warmed")
+        nc.scalar.activation(warmed[:], warm[:], SIGMOID)
+
+        first = keep.tile([P, 1, 2, H], U8, align_bytes=64, name="first")
+        first_i = first[:].rearrange("p e m i -> p (e m i)").bitcast(I32)
+        nc.vector.memset(first_i, 0)
+        first_i = first_i.rearrange("p (e m i) -> p e m i", e=1, m=2)
+        codes = keep.tile([P, T], U32, align_bytes=64, name="codes")
+        scales = keep.tile([P, T], U8, align_bytes=64, name="scales")
+        nc.gpsimd.memset(scales[:], 0)
+        rest = keep.tile([P, E - 1, 2, H], U8, align_bytes=64, name="rest")
+        rest_i = rest[:].rearrange("p e m i -> p (e m i)").bitcast(I32)
+        nc.gpsimd.memset(rest_i, 0)
+        rest_i = rest_i.rearrange("p (e m i) -> p e m i", e=E - 1, m=2)
+        planes2 = keep.tile([P, E, 2, N], U8, align_bytes=64, name="planes2")
+        planes2_i = planes2[:].rearrange("p e s n -> p (e s n)").bitcast(I32)
+        nc.gpsimd.memset(planes2_i, 0)
+        planes2_i = planes2_i.rearrange("p (e s n) -> p e s n", e=E, s=2)
+        windows = []
+        for r in range(N // P):
+            window = keep.tile([P, T], F32, name=f"window{r}")
+            nc.gpsimd.memset(window[:], 0.0)
+            windows.append(window)
+        ident = keep.tile([P, P], F32, name="ident")
+        make_identity(nc, ident[:])
+
+        words0 = keep.tile([P, 2, 2 * H], U8, align_bytes=64, name="words0")
+        words0_i = words0[:].rearrange("p m b -> p (m b)").bitcast(I32).rearrange("p (m b) -> p m b", m=2)
+        later = keep.tile([P, E - 1, 2, 2 * H], U8, align_bytes=64, name="later")
+        later_i = later[:].rearrange("p e m b -> p (e m b)").bitcast(I32).rearrange("p (x b) -> p x b", b=H // 2)
+        words2 = keep.tile([P, E, 2, 2 * N], U8, align_bytes=64, name="words2")
+        words2_i = words2[:].rearrange("p e s b -> p (e s b)").bitcast(I32).rearrange("p (x b) -> p x b", b=N // 2)
+        gates = keep.tile([P, N // P, E * C], F32, name="gates")
+        residual = keep.tile([P, N // P, T], F32, name="residual")
+        nc.gpsimd.memset(later_i[:, :, 0:1], 0)
+        nc.gpsimd.memset(words2_i[:, :, 0:1], 0)
+        nc.gpsimd.memset(gates[:, 0, 0:1], 0.0)
+        nc.gpsimd.memset(residual[:, 0, 0:1], 0.0)
+
+        s1_i, s3_i, s2_i = w1_scales.bitcast(I32), w3_scales.bitcast(I32), w2_scales.bitcast(I32)
+        w1_i, w3_i, w2_i = w1_words.bitcast(I32), w3_words.bitcast(I32), w2_words.bitcast(I32)
+        raws = []
+        t0 = 0
+        for c, width in enumerate(LOADS):
+            raw = keep.tile([P, PACK, width], F32, name=f"raw{c}")
+            nc.sync.dma_start(raw[:], xT.rearrange("(p j) t -> p j t", j=PACK)[:, :, t0 : t0 + width])
+            raws.append((t0, width, raw))
+            t0 += width
+            if c == 0:
+                offsets = keep.tile([P, E * C // 16], U16, name="offsets")
+                nc.sync.dma_start(offsets[:], offs)
+        for r in range(4):
+            for m, src in enumerate((s1_i, s3_i)):
+                nc.sync.dma_start(first_i[r:P:32, 0, m, :], src[0, 0, r:16:4, :])
+        for m, src in enumerate((w1_i, w3_i)):
+            nc.sync.dma_start(words0_i[:, m, :], src[0, 0])
+        nc.sync.dma_start(words2_i[:, 0:2, :], w2_i[0].rearrange("s p b -> p s b"))
+        for r in range(4):
+            nc.sync.dma_start(
+                planes2_i[r:P:32].rearrange("q e s n -> q (e s) n"),
+                s2_i[:, :, r:16:4, :].rearrange("e s q n -> q (e s) n"),
+            )
+        for r in range(4):
+            for m, src in enumerate((s1_i, s3_i)):
+                nc.sync.dma_start(rest_i[r:P:32, :, m, :], src[1:E, 0, r:16:4, :].rearrange("e q i -> q e i"))
+        for e in range(1, E):
+            for m, src in enumerate((w1_i, w3_i)):
+                nc.sync.dma_start(later_i[:, 2 * (e - 1) + m, :], src[e, 0])
+            nc.sync.dma_start(words2_i[:, 2 * e : 2 * e + 2, :], w2_i[e].rearrange("s p b -> p s b"))
+            if e == 1:
+                nc.sync.dma_start(gates[:], gate.rearrange("(r p) j -> p r j", p=P))
+        nc.sync.dma_start(residual[:], xr.rearrange("(r p) t -> p r t", p=P))
+
+        grouped = keep.tile([P, T, PACK], BF16, align_bytes=64, name="grouped")
+        for t0, width, raw in raws:
+            for c in range(0, width, CAST):
+                for copy, a, b in (
+                    (nc.scalar.copy, c, c + SCALAR_TOKENS),
+                    (nc.vector.tensor_copy, c + SCALAR_TOKENS, c + CAST),
+                ):
+                    copy(
+                        grouped[:, t0 + a : t0 + b, :].rearrange("p (c i) j -> p c j i", i=4),
+                        raw[:, :, a:b].rearrange("p j (c i) -> p c j i", i=4),
+                    )
+                cols = slice(t0 + c, t0 + c + CAST)
+                nc.vector.quantize_mx(
+                    out=codes[:, cols].bitcast(FP8X4),
+                    scales=scales[:, cols],
+                    in_=grouped[:, cols, :].rearrange("p t j -> p (t j)"),
+                )
+
+        def slots(e):
+            return offsets[:, e * C // 16 : (e + 1) * C // 16]
+
+        def gather(e):
+            x_codes = keep.tile([P, C], U32, align_bytes=64, name=f"x_codes{e}")
+            x_scales = keep.tile([P, C], U8, align_bytes=64, name=f"x_scales{e}")
+            nc.vector.tensor_copy(x_codes[:], codes[:].indirect(slots(e)))
+            nc.vector.tensor_copy(x_scales[:], scales[:].indirect(slots(e)))
+            return x_codes, x_scales
+
+        def scatter(e, r):
+            nc.vector.tensor_tensor(
+                windows[r][:].indirect(slots(e)), ys[e][:, r, :], gates[:, r, e * C : (e + 1) * C], MULT
+            )
+
+        gathered = [gather(0)]
+        ys = []
+        for e in range(E):
+            x_codes, x_scales = gathered[e]
+            y_bank = psum.tile([P, N // P, C], F32, name="y_bank")
+            for q in range(C // P):
+                cols = slice(q * P, (q + 1) * P)
+                h = ring.tile([P, H], BF16, align_bytes=64, name="h")
+                for s in range(H // HALF):
+                    i_cols = slice(s * HALF, (s + 1) * HALF)
+                    banks = []
+                    for m in range(2):
+                        words = words0[:, m, :] if e == 0 else later[:, e - 1, m, :]
+                        plane = first[:, 0, m, i_cols] if e == 0 else rest[:, e - 1, m, i_cols]
+                        bank = psum.tile([P, HALF], F32, name=f"bank{m}")
+                        nc.tensor.matmul_mx(
+                            out=bank[:],
+                            lhsT=x_codes[:, cols].bitcast(FP8X4),
+                            lhsT_scale=x_scales[:, cols],
+                            rhs=words[:, 2 * s * HALF : 2 * (s + 1) * HALF].bitcast(FP4X4),
+                            rhs_scale=plane,
+                            start=True,
+                            stop=True,
+                        )
+                        banks.append(bank[:].rearrange("p (w u k) -> p u w k", u=2, k=2))
+                    sig = ring.tile([P, HALF], F32, name="sig")
+                    sig_v = sig[:].rearrange("p (u w k) -> p u w k", u=2, k=2)
+                    nc.scalar.activation(sig_v, banks[0], SIGMOID)
+                    nc.vector.tensor_tensor(
+                        h[:, i_cols].rearrange("p (u w k) -> p u w k", u=2, k=2), banks[1], sig_v, MULT
+                    )
+                    if q == 0 and s == 0 and e + 1 < E:
+                        gathered.append(gather(e + 1))
+                turned = psum.tile([P, 2, 2, P], F32, name="turned")
+                for s in range(2):
+                    for u in range(2):
+                        b = 2 * s + u
+                        nc.tensor.transpose(turned[:, s, u, :], h[:].bitcast(F32)[:, b * P : (b + 1) * P], ident[:])
+                hg = ring.tile([P, 2, P, PACK], BF16, align_bytes=64, name="hg")
+                nc.scalar.copy(
+                    hg[:].rearrange("p s c k -> p (s c k)").bitcast(F32).rearrange("p (s c u) -> p s c u", s=2, u=2),
+                    turned[:].rearrange("p s u c -> p s c u"),
+                )
+                h_codes = ring.tile([P, 2 * P], U32, align_bytes=64, name="h_codes")
+                h_scales = ring.tile([P, 2 * P], U8, align_bytes=64, name="h_scales")
+                nc.vector.quantize_mx(
+                    out=h_codes[:].bitcast(FP8X4), scales=h_scales[:], in_=hg[:].rearrange("p s c k -> p (s c k)")
+                )
+                for r in range(N // P):
+                    for s in range(2):
+                        nc.tensor.matmul_mx(
+                            out=y_bank[:, r, cols],
+                            lhsT=words2[:, e, s, 2 * r * P : 2 * (r + 1) * P].bitcast(FP4X4),
+                            lhsT_scale=planes2[:, e, s, r * P : (r + 1) * P],
+                            rhs=h_codes[:, s * P : (s + 1) * P].bitcast(FP8X4),
+                            rhs_scale=h_scales[:, s * P : (s + 1) * P],
+                            start=(s == 0),
+                            stop=(s == 1),
+                        )
+            y = ring.tile([P, N // P, C], F32, name="y")
+            nc.scalar.copy(y[:].rearrange("p r c -> p (r c)"), y_bank[:].rearrange("p r c -> p (r c)"))
+            ys.append(y)
+            if e > 0:
+                for r in range(N // P):
+                    scatter(e - 1, r)
+        for r in range(N // P):
+            scatter(E - 1, r)
+            total = keep.tile([P, T], F32, name=f"total{r}")
+            for a in range(0, T, OUT_PIECE):
+                piece = slice(a, a + OUT_PIECE)
+                nc.vector.tensor_tensor(total[:, piece], windows[r][:, piece], residual[:, r, piece], ADD)
+                nc.sync.dma_start(out[r * P : (r + 1) * P, piece], total[:, piece])

@@ -20,11 +20,11 @@ ADD = mybir.AluOpType.add
 
 P = 128
 PACK = 4
-LOADS = (512, 512, 256)
+LOADS = (512, 640, 128)
 CAST = 256
-SCALAR_TOKENS = 96
+SCALAR_SHARE = 8
 HALF = 512
-OUT_PIECE = 640
+PIECES = ((0, 768), (768, 1280))
 
 
 def tile_moe_res_glu_sigmoid_kernel(
@@ -33,8 +33,8 @@ def tile_moe_res_glu_sigmoid_kernel(
     nc = tc.nc
     with ExitStack() as ctx:
         keep = ctx.enter_context(tc.tile_pool(name="keep", bufs=1))
-        ring = ctx.enter_context(tc.tile_pool(name="ring", bufs=3))
-        psum = ctx.enter_context(tc.psum_pool(name="psum", bufs=2))
+        ring = ctx.enter_context(tc.tile_pool(name="ring", bufs=4))
+        psum = ctx.enter_context(tc.psum_pool(name="psum", bufs=1))
 
         warm = keep.tile([P, 1], F32, name="warm")
         nc.vector.memset(warm[:], 0.0)
@@ -50,16 +50,16 @@ def tile_moe_res_glu_sigmoid_kernel(
         nc.gpsimd.memset(scales[:], 0)
         rest = keep.tile([P, E - 1, 2, H], U8, align_bytes=64, name="rest")
         rest_i = rest[:].rearrange("p e m i -> p (e m i)").bitcast(I32)
-        nc.gpsimd.memset(rest_i, 0)
+        nc.vector.memset(rest_i, 0)
         rest_i = rest_i.rearrange("p (e m i) -> p e m i", e=E - 1, m=2)
         planes2 = keep.tile([P, E, 2, N], U8, align_bytes=64, name="planes2")
         planes2_i = planes2[:].rearrange("p e s n -> p (e s n)").bitcast(I32)
-        nc.gpsimd.memset(planes2_i, 0)
+        nc.vector.memset(planes2_i, 0)
         planes2_i = planes2_i.rearrange("p (e s n) -> p e s n", e=E, s=2)
         windows = []
         for r in range(N // P):
             window = keep.tile([P, T], F32, name=f"window{r}")
-            nc.gpsimd.memset(window[:], 0.0)
+            (nc.gpsimd if r == 0 else nc.vector).memset(window[:], 0.0)
             windows.append(window)
         ident = keep.tile([P, P], F32, name="ident")
         make_identity(nc, ident[:])
@@ -114,15 +114,14 @@ def tile_moe_res_glu_sigmoid_kernel(
         grouped = keep.tile([P, T, PACK], BF16, align_bytes=64, name="grouped")
         for t0, width, raw in raws:
             for c in range(0, width, CAST):
-                for copy, a, b in (
-                    (nc.scalar.copy, c, c + SCALAR_TOKENS),
-                    (nc.vector.tensor_copy, c + SCALAR_TOKENS, c + CAST),
-                ):
+                end = min(c + CAST, width)
+                cut = c + 3 * (end - c) // SCALAR_SHARE
+                for copy, a, b in ((nc.scalar.copy, c, cut), (nc.vector.tensor_copy, cut, end)):
                     copy(
                         grouped[:, t0 + a : t0 + b, :].rearrange("p (c i) j -> p c j i", i=4),
                         raw[:, :, a:b].rearrange("p j (c i) -> p c j i", i=4),
                     )
-                cols = slice(t0 + c, t0 + c + CAST)
+                cols = slice(t0 + c, t0 + end)
                 nc.vector.quantize_mx(
                     out=codes[:, cols].bitcast(FP8X4),
                     scales=scales[:, cols],
@@ -158,7 +157,7 @@ def tile_moe_res_glu_sigmoid_kernel(
                     for m in range(2):
                         words = words0[:, m, :] if e == 0 else later[:, e - 1, m, :]
                         plane = first[:, 0, m, i_cols] if e == 0 else rest[:, e - 1, m, i_cols]
-                        bank = psum.tile([P, HALF], F32, name=f"bank{m}")
+                        bank = psum.tile([P, HALF], F32, name=f"bank{m}", bufs=2 + m)
                         nc.tensor.matmul_mx(
                             out=bank[:],
                             lhsT=x_codes[:, cols].bitcast(FP8X4),
@@ -175,9 +174,9 @@ def tile_moe_res_glu_sigmoid_kernel(
                     nc.vector.tensor_tensor(
                         h[:, i_cols].rearrange("p (u w k) -> p u w k", u=2, k=2), banks[1], sig_v, MULT
                     )
-                    if q == 0 and s == 0 and e + 1 < E:
-                        gathered.append(gather(e + 1))
-                turned = psum.tile([P, 2, 2, P], F32, name="turned")
+                    if len(gathered) < E:
+                        gathered.append(gather(len(gathered)))
+                turned = psum.tile([P, 2, 2, P], F32, name="turned", bufs=2)
                 for s in range(2):
                     for u in range(2):
                         b = 2 * s + u
@@ -203,16 +202,18 @@ def tile_moe_res_glu_sigmoid_kernel(
                             start=(s == 0),
                             stop=(s == 1),
                         )
-            y = ring.tile([P, N // P, C], F32, name="y")
+            y = keep.tile([P, N // P, C], F32, name=f"y{e}")
             nc.scalar.copy(y[:].rearrange("p r c -> p (r c)"), y_bank[:].rearrange("p r c -> p (r c)"))
             ys.append(y)
-            if e > 0:
+            if e > 1:
                 for r in range(N // P):
-                    scatter(e - 1, r)
+                    scatter(e - 2, r)
+        for r in range(N // P):
+            scatter(E - 2, r)
         for r in range(N // P):
             scatter(E - 1, r)
             total = keep.tile([P, T], F32, name=f"total{r}")
-            for a in range(0, T, OUT_PIECE):
-                piece = slice(a, a + OUT_PIECE)
+            for a, b in PIECES:
+                piece = slice(a, b)
                 nc.vector.tensor_tensor(total[:, piece], windows[r][:, piece], residual[:, r, piece], ADD)
                 nc.sync.dma_start(out[r * P : (r + 1) * P, piece], total[:, piece])

@@ -24,7 +24,17 @@ LOADS = (512, 640, 128)
 CAST = 256
 SCALAR_SHARE = 8
 HALF = 512
-PIECES = ((0, 768), (768, 1280))
+GATHERS = (0, 160, 512, 768, 1024)
+SCATTERS = (0, 256, 512, 704, 864, 1024)
+AFTER_PRODUCT = {
+    (1, 1, 1): ((0, 0),),
+    (2, 0, 1): ((0, 1),),
+    (2, 1, 1): ((1, 0),),
+    (3, 0, 1): ((1, 1),),
+    (3, 1, 1): ((2, 0), (2, 1)),
+}
+AFTER_TURN = {(3, 1): ((3, 0), (3, 1))}
+PIECES = (((0, 640), (640, 1280)), ((0, 512), (512, 1024), (1024, 1280)))
 
 
 def tile_moe_res_glu_sigmoid_kernel(
@@ -128,28 +138,33 @@ def tile_moe_res_glu_sigmoid_kernel(
                     in_=grouped[:, cols, :].rearrange("p t j -> p (t j)"),
                 )
 
-        def slots(e):
-            return offsets[:, e * C // 16 : (e + 1) * C // 16]
+        x_codes = keep.tile([P, E * C], U32, align_bytes=64, name="x_codes")
+        x_scales = keep.tile([P, E * C], U8, align_bytes=64, name="x_scales")
+        y = keep.tile([P, N // P, E * C], F32, name="y")
 
-        def gather(e):
-            x_codes = keep.tile([P, C], U32, align_bytes=64, name=f"x_codes{e}")
-            x_scales = keep.tile([P, C], U8, align_bytes=64, name=f"x_scales{e}")
-            nc.vector.tensor_copy(x_codes[:], codes[:].indirect(slots(e)))
-            nc.vector.tensor_copy(x_scales[:], scales[:].indirect(slots(e)))
-            return x_codes, x_scales
+        def gather(g):
+            part = slice(GATHERS[g], GATHERS[g + 1])
+            entries = offsets[:, part.start // 16 : part.stop // 16]
+            nc.vector.tensor_copy(x_codes[:, part], codes[:].indirect(entries))
+            nc.vector.tensor_copy(x_scales[:, part], scales[:].indirect(entries))
 
-        def scatter(e, r):
-            nc.vector.tensor_tensor(
-                windows[r][:].indirect(slots(e)), ys[e][:, r, :], gates[:, r, e * C : (e + 1) * C], MULT
-            )
+        def scatter(g, r):
+            part = slice(SCATTERS[g], SCATTERS[g + 1])
+            entries = offsets[:, part.start // 16 : part.stop // 16]
+            nc.vector.tensor_tensor(windows[r][:].indirect(entries), y[:, r, part], gates[:, r, part], MULT)
 
-        gathered = [gather(0)]
-        ys = []
+        token = keep.tile([P, 10], F32, name="token")
+
+        def scatter_after(event, later):
+            for g, r in later:
+                nc.gpsimd.tensor_tensor(token[:, 2 * g + r : 2 * g + r + 1], windows[r][:, 0:1], event, ADD)
+                scatter(g, r)
+
+        gather(0)
+        gather(1)
         for e in range(E):
-            x_codes, x_scales = gathered[e]
-            y_bank = psum.tile([P, N // P, C], F32, name="y_bank")
             for q in range(C // P):
-                cols = slice(q * P, (q + 1) * P)
+                slots = slice(e * C + q * P, e * C + (q + 1) * P)
                 h = ring.tile([P, H], BF16, align_bytes=64, name="h")
                 for s in range(H // HALF):
                     i_cols = slice(s * HALF, (s + 1) * HALF)
@@ -160,8 +175,8 @@ def tile_moe_res_glu_sigmoid_kernel(
                         bank = psum.tile([P, HALF], F32, name=f"bank{m}", bufs=2 + m)
                         nc.tensor.matmul_mx(
                             out=bank[:],
-                            lhsT=x_codes[:, cols].bitcast(FP8X4),
-                            lhsT_scale=x_scales[:, cols],
+                            lhsT=x_codes[:, slots].bitcast(FP8X4),
+                            lhsT_scale=x_scales[:, slots],
                             rhs=words[:, 2 * s * HALF : 2 * (s + 1) * HALF].bitcast(FP4X4),
                             rhs_scale=plane,
                             start=True,
@@ -174,8 +189,9 @@ def tile_moe_res_glu_sigmoid_kernel(
                     nc.vector.tensor_tensor(
                         h[:, i_cols].rearrange("p (u w k) -> p u w k", u=2, k=2), banks[1], sig_v, MULT
                     )
-                    if len(gathered) < E:
-                        gathered.append(gather(len(gathered)))
+                    if e == 0 and q == 1:
+                        gather(2 + s)
+                    scatter_after(h[:, s * HALF : s * HALF + 1], AFTER_PRODUCT.get((e, q, s), ()))
                 turned = psum.tile([P, 2, 2, P], F32, name="turned", bufs=2)
                 for s in range(2):
                     for u in range(2):
@@ -186,15 +202,17 @@ def tile_moe_res_glu_sigmoid_kernel(
                     hg[:].rearrange("p s c k -> p (s c k)").bitcast(F32).rearrange("p (s c u) -> p s c u", s=2, u=2),
                     turned[:].rearrange("p s u c -> p s c u"),
                 )
+                scatter_after(hg[:, 0, 0, 0:1], AFTER_TURN.get((e, q), ()))
                 h_codes = ring.tile([P, 2 * P], U32, align_bytes=64, name="h_codes")
                 h_scales = ring.tile([P, 2 * P], U8, align_bytes=64, name="h_scales")
                 nc.vector.quantize_mx(
                     out=h_codes[:].bitcast(FP8X4), scales=h_scales[:], in_=hg[:].rearrange("p s c k -> p (s c k)")
                 )
+                y_bank = psum.tile([P, N // P, P], F32, name="y_bank")
                 for r in range(N // P):
                     for s in range(2):
                         nc.tensor.matmul_mx(
-                            out=y_bank[:, r, cols],
+                            out=y_bank[:, r, :],
                             lhsT=words2[:, e, s, 2 * r * P : 2 * (r + 1) * P].bitcast(FP4X4),
                             lhsT_scale=planes2[:, e, s, r * P : (r + 1) * P],
                             rhs=h_codes[:, s * P : (s + 1) * P].bitcast(FP8X4),
@@ -202,18 +220,11 @@ def tile_moe_res_glu_sigmoid_kernel(
                             start=(s == 0),
                             stop=(s == 1),
                         )
-            y = keep.tile([P, N // P, C], F32, name=f"y{e}")
-            nc.scalar.copy(y[:].rearrange("p r c -> p (r c)"), y_bank[:].rearrange("p r c -> p (r c)"))
-            ys.append(y)
-            if e > 1:
-                for r in range(N // P):
-                    scatter(e - 2, r)
+                nc.scalar.copy(y[:, :, slots], y_bank[:])
         for r in range(N // P):
-            scatter(E - 2, r)
-        for r in range(N // P):
-            scatter(E - 1, r)
+            scatter(4, r)
             total = keep.tile([P, T], F32, name=f"total{r}")
-            for a, b in PIECES:
+            for a, b in PIECES[r]:
                 piece = slice(a, b)
                 nc.vector.tensor_tensor(total[:, piece], windows[r][:, piece], residual[:, r, piece], ADD)
                 nc.sync.dma_start(out[r * P : (r + 1) * P, piece], total[:, piece])

@@ -102,8 +102,10 @@ def tile_moe_res_glu_sigmoid_kernel(
         for r in range(4):
             for m, src in enumerate((s1_i, s3_i)):
                 nc.sync.dma_start(first_i[r:P:32, 0, m, :], src[0, 0, r:16:4, :])
-        for m, src in enumerate((w1_i, w3_i)):
-            nc.sync.dma_start(words0_i[:, m, :], src[0, 0])
+        for s in range(2):
+            part = slice(s * HALF // 2, (s + 1) * HALF // 2)
+            for m, src in enumerate((w1_i, w3_i)):
+                nc.sync.dma_start(words0_i[:, m, part], src[0, 0][:, part])
         nc.sync.dma_start(words2_i[:, 0:2, :], w2_i[0].rearrange("s p b -> p s b"))
         for r in range(4):
             nc.sync.dma_start(
@@ -172,7 +174,7 @@ def tile_moe_res_glu_sigmoid_kernel(
                     for m in range(2):
                         words = words0[:, m, :] if e == 0 else later[:, e - 1, m, :]
                         plane = first[:, 0, m, i_cols] if e == 0 else rest[:, e - 1, m, i_cols]
-                        bank = psum.tile([P, HALF], F32, name=f"bank{m}", bufs=2 + m)
+                        bank = psum.tile([P, HALF], F32, name=f"bank{m}", bufs=3)
                         nc.tensor.matmul_mx(
                             out=bank[:],
                             lhsT=x_codes[:, slots].bitcast(FP8X4),
@@ -192,7 +194,7 @@ def tile_moe_res_glu_sigmoid_kernel(
                     if e == 0 and q == 1:
                         gather(2 + s)
                     scatter_after(h[:, s * HALF : s * HALF + 1], AFTER_PRODUCT.get((e, q, s), ()))
-                turned = psum.tile([P, 2, 2, P], F32, name="turned", bufs=2)
+                turned = psum.tile([P, 2, 2, P], F32, name="turned")
                 for s in range(2):
                     for u in range(2):
                         b = 2 * s + u

from contextlib import ExitStack

import concourse.mybir as mybir
from concourse.masks import make_identity

K, T, E, C, H, N = 512, 1280, 4, 256, 1024, 256
FLOPS = 2 * E * C * (2 * K * H + H * N)

F32 = mybir.dt.float32
BF16 = mybir.dt.bfloat16
I32 = mybir.dt.int32
U32 = mybir.dt.uint32
U16 = mybir.dt.uint16
U8 = mybir.dt.uint8
FP8X4 = mybir.dt.float8_e4m3fn_x4
FP4X4 = mybir.dt.float4_e2m1fn_x4
SIGMOID = mybir.ActivationFunctionType.Sigmoid
MULT = mybir.AluOpType.mult
ADD = mybir.AluOpType.add

P = 128
PACK = 4
LOADS = (512, 640, 128)
CAST = 256
SCALAR_SHARE = 8
HALF = 512
GATHERS = (0, 160, 512, 768, 1024)
SCATTERS = (0, 256, 512, 704, 864, 1024)
AFTER_PRODUCT = {
    (1, 1, 1): ((0, 0),),
    (2, 0, 1): ((0, 1),),
    (2, 1, 1): ((1, 0),),
    (3, 0, 1): ((1, 1),),
    (3, 1, 1): ((2, 0), (2, 1)),
}
AFTER_TURN = {(3, 1): ((3, 0), (3, 1))}
PIECES = (((0, 640), (640, 1280)), ((0, 512), (512, 1024), (1024, 1280)))


def tile_moe_res_glu_sigmoid_kernel(
    tc, xT, xr, w1_words, w1_scales, w3_words, w3_scales, w2_words, w2_scales, gate, offs, out
):
    nc = tc.nc
    with ExitStack() as ctx:
        keep = ctx.enter_context(tc.tile_pool(name="keep", bufs=1))
        ring = ctx.enter_context(tc.tile_pool(name="ring", bufs=4))
        psum = ctx.enter_context(tc.psum_pool(name="psum", bufs=1))

        warm = keep.tile([P, 1], F32, name="warm")
        nc.vector.memset(warm[:], 0.0)
        warmed = keep.tile([P, 1], F32, name="warmed")
        nc.scalar.activation(warmed[:], warm[:], SIGMOID)

        first = keep.tile([P, 1, 2, H], U8, align_bytes=64, name="first")
        first_i = first[:].rearrange("p e m i -> p (e m i)").bitcast(I32)
        nc.vector.memset(first_i, 0)
        first_i = first_i.rearrange("p (e m i) -> p e m i", e=1, m=2)
        codes = keep.tile([P, T], U32, align_bytes=64, name="codes")
        scales = keep.tile([P, T], U8, align_bytes=64, name="scales")
        nc.gpsimd.memset(scales[:], 0)
        rest = keep.tile([P, E - 1, 2, H], U8, align_bytes=64, name="rest")
        rest_i = rest[:].rearrange("p e m i -> p (e m i)").bitcast(I32)
        nc.vector.memset(rest_i, 0)
        rest_i = rest_i.rearrange("p (e m i) -> p e m i", e=E - 1, m=2)
        planes2 = keep.tile([P, E, 2, N], U8, align_bytes=64, name="planes2")
        planes2_i = planes2[:].rearrange("p e s n -> p (e s n)").bitcast(I32)
        nc.vector.memset(planes2_i, 0)
        planes2_i = planes2_i.rearrange("p (e s n) -> p e s n", e=E, s=2)
        windows = []
        for r in range(N // P):
            window = keep.tile([P, T], F32, name=f"window{r}")
            (nc.gpsimd if r == 0 else nc.vector).memset(window[:], 0.0)
            windows.append(window)
        ident = keep.tile([P, P], F32, name="ident")
        make_identity(nc, ident[:])

        words0 = keep.tile([P, 2, 2 * H], U8, align_bytes=64, name="words0")
        words0_i = words0[:].rearrange("p m b -> p (m b)").bitcast(I32).rearrange("p (m b) -> p m b", m=2)
        later = keep.tile([P, E - 1, 2, 2 * H], U8, align_bytes=64, name="later")
        later_i = later[:].rearrange("p e m b -> p (e m b)").bitcast(I32).rearrange("p (x b) -> p x b", b=H // 2)
        words2 = keep.tile([P, E, 2, 2 * N], U8, align_bytes=64, name="words2")
        words2_i = words2[:].rearrange("p e s b -> p (e s b)").bitcast(I32).rearrange("p (x b) -> p x b", b=N // 2)
        gates = keep.tile([P, N // P, E * C], F32, name="gates")
        residual = keep.tile([P, N // P, T], F32, name="residual")
        nc.gpsimd.memset(later_i[:, :, 0:1], 0)
        nc.gpsimd.memset(words2_i[:, :, 0:1], 0)
        nc.gpsimd.memset(gates[:, 0, 0:1], 0.0)
        nc.gpsimd.memset(residual[:, 0, 0:1], 0.0)

        s1_i, s3_i, s2_i = w1_scales.bitcast(I32), w3_scales.bitcast(I32), w2_scales.bitcast(I32)
        w1_i, w3_i, w2_i = w1_words.bitcast(I32), w3_words.bitcast(I32), w2_words.bitcast(I32)
        raws = []
        t0 = 0
        for c, width in enumerate(LOADS):
            raw = keep.tile([P, PACK, width], F32, name=f"raw{c}")
            nc.sync.dma_start(raw[:], xT.rearrange("(p j) t -> p j t", j=PACK)[:, :, t0 : t0 + width])
            raws.append((t0, width, raw))
            t0 += width
            if c == 0:
                offsets = keep.tile([P, E * C // 16], U16, name="offsets")
                nc.sync.dma_start(offsets[:], offs)
        for r in range(4):
            for m, src in enumerate((s1_i, s3_i)):
                nc.sync.dma_start(first_i[r:P:32, 0, m, :], src[0, 0, r:16:4, :])
        for s in range(2):
            part = slice(s * HALF // 2, (s + 1) * HALF // 2)
            for m, src in enumerate((w1_i, w3_i)):
                nc.sync.dma_start(words0_i[:, m, part], src[0, 0][:, part])
        nc.sync.dma_start(words2_i[:, 0:2, :], w2_i[0].rearrange("s p b -> p s b"))
        for r in range(4):
            nc.sync.dma_start(
                planes2_i[r:P:32].rearrange("q e s n -> q (e s) n"),
                s2_i[:, :, r:16:4, :].rearrange("e s q n -> q (e s) n"),
            )
        for r in range(4):
            for m, src in enumerate((s1_i, s3_i)):
                nc.sync.dma_start(rest_i[r:P:32, :, m, :], src[1:E, 0, r:16:4, :].rearrange("e q i -> q e i"))
        for e in range(1, E):
            for m, src in enumerate((w1_i, w3_i)):
                nc.sync.dma_start(later_i[:, 2 * (e - 1) + m, :], src[e, 0])
            nc.sync.dma_start(words2_i[:, 2 * e : 2 * e + 2, :], w2_i[e].rearrange("s p b -> p s b"))
            if e == 1:
                nc.sync.dma_start(gates[:], gate.rearrange("(r p) j -> p r j", p=P))
        nc.sync.dma_start(residual[:], xr.rearrange("(r p) t -> p r t", p=P))

        grouped = keep.tile([P, T, PACK], BF16, align_bytes=64, name="grouped")
        for t0, width, raw in raws:
            for c in range(0, width, CAST):
                end = min(c + CAST, width)
                cut = c + 3 * (end - c) // SCALAR_SHARE
                for copy, a, b in ((nc.scalar.copy, c, cut), (nc.vector.tensor_copy, cut, end)):
                    copy(
                        grouped[:, t0 + a : t0 + b, :].rearrange("p (c i) j -> p c j i", i=4),
                        raw[:, :, a:b].rearrange("p j (c i) -> p c j i", i=4),
                    )
                cols = slice(t0 + c, t0 + end)
                nc.vector.quantize_mx(
                    out=codes[:, cols].bitcast(FP8X4),
                    scales=scales[:, cols],
                    in_=grouped[:, cols, :].rearrange("p t j -> p (t j)"),
                )

        x_codes = keep.tile([P, E * C], U32, align_bytes=64, name="x_codes")
        x_scales = keep.tile([P, E * C], U8, align_bytes=64, name="x_scales")
        y = keep.tile([P, N // P, E * C], F32, name="y")

        def gather(g):
            part = slice(GATHERS[g], GATHERS[g + 1])
            entries = offsets[:, part.start // 16 : part.stop // 16]
            nc.vector.tensor_copy(x_codes[:, part], codes[:].indirect(entries))
            nc.vector.tensor_copy(x_scales[:, part], scales[:].indirect(entries))

        def scatter(g, r):
            part = slice(SCATTERS[g], SCATTERS[g + 1])
            entries = offsets[:, part.start // 16 : part.stop // 16]
            nc.vector.tensor_tensor(windows[r][:].indirect(entries), y[:, r, part], gates[:, r, part], MULT)

        token = keep.tile([P, 10], F32, name="token")

        def scatter_after(event, later):
            for g, r in later:
                nc.gpsimd.tensor_tensor(token[:, 2 * g + r : 2 * g + r + 1], windows[r][:, 0:1], event, ADD)
                scatter(g, r)

        gather(0)
        gather(1)
        for e in range(E):
            for q in range(C // P):
                slots = slice(e * C + q * P, e * C + (q + 1) * P)
                h = ring.tile([P, H], BF16, align_bytes=64, name="h")
                for s in range(H // HALF):
                    i_cols = slice(s * HALF, (s + 1) * HALF)
                    banks = []
                    for m in range(2):
                        words = words0[:, m, :] if e == 0 else later[:, e - 1, m, :]
                        plane = first[:, 0, m, i_cols] if e == 0 else rest[:, e - 1, m, i_cols]
                        bank = psum.tile([P, HALF], F32, name=f"bank{m}", bufs=3)
                        nc.tensor.matmul_mx(
                            out=bank[:],
                            lhsT=x_codes[:, slots].bitcast(FP8X4),
                            lhsT_scale=x_scales[:, slots],
                            rhs=words[:, 2 * s * HALF : 2 * (s + 1) * HALF].bitcast(FP4X4),
                            rhs_scale=plane,
                            start=True,
                            stop=True,
                        )
                        banks.append(bank[:].rearrange("p (w u k) -> p u w k", u=2, k=2))
                    sig = ring.tile([P, HALF], F32, name="sig")
                    sig_v = sig[:].rearrange("p (u w k) -> p u w k", u=2, k=2)
                    nc.scalar.activation(sig_v, banks[0], SIGMOID)
                    nc.vector.tensor_tensor(
                        h[:, i_cols].rearrange("p (u w k) -> p u w k", u=2, k=2), banks[1], sig_v, MULT
                    )
                    if e == 0 and q == 1:
                        gather(2 + s)
                    scatter_after(h[:, s * HALF : s * HALF + 1], AFTER_PRODUCT.get((e, q, s), ()))
                turned = psum.tile([P, 2, 2, P], F32, name="turned")
                for s in range(2):
                    for u in range(2):
                        b = 2 * s + u
                        nc.tensor.transpose(turned[:, s, u, :], h[:].bitcast(F32)[:, b * P : (b + 1) * P], ident[:])
                hg = ring.tile([P, 2, P, PACK], BF16, align_bytes=64, name="hg")
                nc.scalar.copy(
                    hg[:].rearrange("p s c k -> p (s c k)").bitcast(F32).rearrange("p (s c u) -> p s c u", s=2, u=2),
                    turned[:].rearrange("p s u c -> p s c u"),
                )
                scatter_after(hg[:, 0, 0, 0:1], AFTER_TURN.get((e, q), ()))
                h_codes = ring.tile([P, 2 * P], U32, align_bytes=64, name="h_codes")
                h_scales = ring.tile([P, 2 * P], U8, align_bytes=64, name="h_scales")
                nc.vector.quantize_mx(
                    out=h_codes[:].bitcast(FP8X4), scales=h_scales[:], in_=hg[:].rearrange("p s c k -> p (s c k)")
                )
                y_bank = psum.tile([P, N // P, P], F32, name="y_bank")
                for r in range(N // P):
                    for s in range(2):
                        nc.tensor.matmul_mx(
                            out=y_bank[:, r, :],
                            lhsT=words2[:, e, s, 2 * r * P : 2 * (r + 1) * P].bitcast(FP4X4),
                            lhsT_scale=planes2[:, e, s, r * P : (r + 1) * P],
                            rhs=h_codes[:, s * P : (s + 1) * P].bitcast(FP8X4),
                            rhs_scale=h_scales[:, s * P : (s + 1) * P],
                            start=(s == 0),
                            stop=(s == 1),
                        )
                nc.scalar.copy(y[:, :, slots], y_bank[:])
        for r in range(N // P):
            scatter(4, r)
            total = keep.tile([P, T], F32, name=f"total{r}")
            for a, b in PIECES[r]:
                piece = slice(a, b)
                nc.vector.tensor_tensor(total[:, piece], windows[r][:, piece], residual[:, r, piece], ADD)
                nc.sync.dma_start(out[r * P : (r + 1) * P, piece], total[:, piece])
